import numpy as np
import ml_dtypes


def mxq(x, axis, fmt="e4m3"):
    dtype, down = {"e4m3": (ml_dtypes.float8_e4m3fn, 7), "e5m2": (ml_dtypes.float8_e5m2, 14)}[fmt]
    v = np.moveaxis(np.asarray(x, np.float32).astype(ml_dtypes.bfloat16).astype(np.float64), axis, -1)
    blocks = v.reshape(v.shape[:-1] + (-1, 32))
    amax = np.abs(blocks).max(-1, keepdims=True)
    byte = np.maximum(np.where(amax > 0, np.frexp(amax)[1] - 1 + 127, 0) - down, 1)
    scale = np.exp2(byte - 127.0)
    codes = (blocks / scale).astype(np.float32).astype(dtype).astype(np.float64)
    return np.moveaxis((codes * scale).reshape(v.shape), -1, axis)


WIDE = False


def mx_kscale(k):
    if not WIDE:
        return np.ones(k)
    levels = np.array([30, -30])
    if k % 512:
        return np.exp2(np.random.permutation(np.resize(levels, k // 32))).repeat(32)
    a = np.empty((k // 512, 16))
    for p in range(k // 512):
        a[p, :8] = np.random.permutation(np.resize(levels, 8))
        for g in range(8):
            far = levels[np.abs(levels - a[p, g]) >= 10]
            a[p, g + 8] = far[np.random.randint(len(far))]
    return np.exp2(a.ravel()).repeat(32)


def f64(x):
    return np.asarray(x).astype(np.float64)


def striped(idx):
    return np.tile(np.asarray(idx).reshape(-1, 16).T, (8, 1)).astype(np.uint16)


def unstriped(offs):
    return offs[:16].T.reshape(-1).astype(np.int64)


def striped8(idx):
    return np.asarray(idx).reshape(8, -1, 16).transpose(0, 2, 1).reshape(128, -1).astype(np.uint16)


def unstriped8(offs):
    return offs.reshape(8, 16, -1).transpose(0, 2, 1).reshape(8, -1).astype(np.int64)


def pick8(x, idx, run):
    r = np.arange(len(x))
    return x[r[:, None], idx[r % (8 * run) // run]]


E2M1 = np.array([0.0, 0.5, 1.0, 1.5, 2.0, 3.0, 4.0, 6.0, -0.0, -0.5, -1.0, -1.5, -2.0, -3.0, -4.0, -6.0])


def pack_weight(w, fmt):
    k, n = w.shape
    w = f64(np.asarray(w, np.float32).astype(ml_dtypes.bfloat16)).reshape(k // 32, 32, n)
    amax = np.abs(w).max(1)
    if fmt in ("e4m3", "e5m2"):
        byte = np.frexp(amax)[1] - 1 + 127 - (7 if fmt == "e4m3" else 14)
    else:
        mant, ex = np.frexp(amax / 6.0)
        byte = np.where(mant > 0.5, ex, ex - 1) + 127
    byte = np.clip(np.where(amax > 0, byte, 1), 1, 254)
    scaled = (w * np.exp2(127.0 - byte)[:, None, :]).reshape(k, n).astype(np.float32)
    by_word = np.ascontiguousarray(scaled.reshape(k // 512, 128, 4, n).transpose(0, 1, 3, 2))
    if fmt in ("e4m3", "e5m2"):
        words = by_word.astype(ml_dtypes.float8_e4m3fn if fmt == "e4m3" else ml_dtypes.float8_e5m2).view(np.uint8)
    else:
        c = by_word.astype(ml_dtypes.float4_e2m1fn).view(np.uint8) & 0xF
        words = (c[..., 0::2] | (c[..., 1::2] << 4)).reshape(k // 512, 128, 2 * n)
    return np.ascontiguousarray(words), np.ascontiguousarray(byte.astype(np.uint8).reshape(k // 512, 16, n))


def unpack_weight(words, scales, fmt):
    g, _, n = scales.shape
    words = np.ascontiguousarray(words).reshape(g, 128, n, -1)
    if fmt in ("e4m3", "e5m2"):
        vals = words.view(ml_dtypes.float8_e4m3fn if fmt == "e4m3" else ml_dtypes.float8_e5m2).astype(np.float64)
    else:
        nib = np.empty((g, 128, n, 4), np.uint8)
        nib[..., 0::2] = words & 0xF
        nib[..., 1::2] = words >> 4
        vals = E2M1[nib]
    vals = vals * np.repeat(np.exp2(scales.astype(np.float64) - 127.0), 8, axis=1)[..., None]
    return vals.transpose(0, 1, 3, 2).reshape(g * 512, n)


K, T, J, R, F, Z, C, O, N, S, E = 512, 1024, 256, 512, 512, 1024, 512, 128, 256, 1024, 1024


def setup_inputs():
    n = np.random.standard_normal
    idx = np.random.permutation(T)[:J]
    idx2 = np.random.permutation(Z)[:J]
    idx3 = np.stack([np.random.permutation(C)[:J] for _ in range(8)])
    idx4 = np.random.permutation(C)[:O]
    idx5 = np.random.permutation(C)[:O]
    idx6 = np.random.permutation(S)[:N]
    idx7 = np.random.permutation(E)[:O]
    fk = mx_kscale(K)
    ff = mx_kscale(F)
    fr = mx_kscale(R)
    xtp = pack_weight(n((K, T)) / fk[:, None], "e4m3")
    xop = pack_weight(n((F, Z)) / ff[:, None], "e2m1")
    wp = pack_weight(n((K, R)) * 1 / np.sqrt(K) * fk[:, None] * fr, "e2m1")
    w0p = pack_weight(n((F, R)) * 1 / np.sqrt(F) * ff[:, None] * fr, "e5m2")
    vsp = pack_weight(n((R, S)) * 1 / np.sqrt(R) / fr[:, None], "e5m2")
    return {
        "xt_words": xtp[0],
        "xt_scales": xtp[1],
        "xo_words": xop[0],
        "xo_scales": xop[1],
        "w_words": wp[0],
        "w_scales": wp[1],
        "w0_words": w0p[0],
        "w0_scales": w0p[1],
        "sa": (np.random.uniform(0.5, 1.6, (R, 1))).astype(np.float32),
        "sb": (np.random.uniform(0.5, 1.6, (R, 1))).astype(np.float32),
        "vs_words": vsp[0],
        "vs_scales": vsp[1],
        "offs": striped(idx),
        "offs2": striped(idx2),
        "offs3": striped8(idx3),
        "offs4": striped(idx4),
        "offs5": striped(idx5),
        "offs6": striped(idx6),
        "offs7": striped(idx7),
    }


def reference(xt_words, xt_scales, xo_words, xo_scales, w_words, w_scales, w0_words, w0_scales, sa, sb, vs_words, vs_scales, offs, offs2, offs3, offs4, offs5, offs6, offs7):
    idx = unstriped(offs)
    idx2 = unstriped(offs2)
    idx3 = unstriped8(offs3)
    idx4 = unstriped(offs4)
    idx5 = unstriped(offs5)
    idx6 = unstriped(offs6)
    idx7 = unstriped(offs7)
    xtu = unpack_weight(xt_words, xt_scales, "e4m3")
    xou = unpack_weight(xo_words, xo_scales, "e2m1")
    wu = unpack_weight(w_words, w_scales, "e2m1")
    w0u = unpack_weight(w0_words, w0_scales, "e5m2")
    vsu = unpack_weight(vs_words, vs_scales, "e5m2")
    xtidxg = xtu[:, idx]
    xoidx2g = xou[:, idx2]
    a = wu.T @ xtidxg + w0u.T @ xoidx2g
    pw = np.zeros((R, C))
    pw[np.arange(R)[:, None], idx3[np.arange(R) % 512 // 64]] = a
    hid = np.abs(pw[:, idx4] * f64(sa) - pw[:, idx5] * f64(sb))
    vsidx6g = vsu[:, idx6]
    hidq = mxq(hid, 0, "e4m3")
    p = vsidx6g.T @ hidq
    y = np.zeros((N, E))
    y[:, idx7] = p
    return y

@@ -1,0 +1,183 @@
+from contextlib import ExitStack
+
+import concourse.mybir as mybir
+
+F32 = mybir.dt.float32
+BF16 = mybir.dt.bfloat16
+I32 = mybir.dt.int32
+U32 = mybir.dt.uint32
+U16 = mybir.dt.uint16
+U8 = mybir.dt.uint8
+E4M3 = mybir.dt.float8_e4m3fn_x4
+E5M2 = mybir.dt.float8_e5m2_x4
+E2M1 = mybir.dt.float4_e2m1fn_x4
+COPY = mybir.ActivationFunctionType.Copy
+ALU = mybir.AluOpType
+
+P = 128
+K, T, J, R, F, Z, C, O, N, S, E = 512, 1024, 256, 512, 512, 1024, 512, 128, 256, 1024, 1024
+FLOPS = 2 * K * R * J + 2 * F * R * J + 2 * R * N * O
+H = J // 2
+
+
+def tile_list_ownboard_bank_store_scattered_kernel(
+    tc, xt_words, xt_scales, xo_words, xo_scales, w_words, w_scales, w0_words, w0_scales,
+    sa, sb, vs_words, vs_scales, offs, offs2, offs3, offs4, offs5, offs6, offs7, out
+):
+    nc = tc.nc
+    with ExitStack() as ctx:
+        lists = ctx.enter_context(tc.tile_pool(name="lists", bufs=1))
+        sb_pool = ctx.enter_context(tc.tile_pool(name="sbuf", bufs=1))
+        psum = ctx.enter_context(tc.psum_pool(name="psum", bufs=1))
+
+        def tile(shape, dtype, name, tag=None):
+            return sb_pool.tile(shape, dtype, name=name, tag=tag or name, align_bytes=64)
+
+        def load_list(src, name):
+            t = lists.tile(list(src.shape), U16, name=name)
+            nc.sync.dma_start(t[:], src)
+            return t
+
+        def words8(src):
+            return src[0].rearrange("p n b -> p (n b)").bitcast(I32)
+
+        def lane_rows(src, r):
+            return src[0].bitcast(I32)[r:16:4, :]
+
+        xo_stage = tile([P, 2, Z // 4], I32, "xo_stage")
+        xt_plane = tile([P, T], U8, "xt_plane")
+        xo_plane = tile([P, Z], U8, "xo_plane")
+        w_plane = tile([P, 2, R], U8, "w_plane")
+        nc.vector.memset(xo_stage[64:P], 0)
+        nc.vector.memset(xt_plane[:].bitcast(I32), 0)
+        nc.vector.memset(w_plane[:].bitcast(I32), 0)
+
+        w_raw = tile([P, R], U16, "w_raw")
+        w0_raw = tile([P, R], U32, "w0_raw")
+        xt_win = tile([P, T], U32, "xt_win", "page0")
+        xo_win = tile([P, Z], U16, "xo_win", "page1")
+        w_stage = tile([4, 4, 2, R // 4], I32, "w_stage")
+
+        nc.sync.dma_start(w_stage[:, :, 0, :], w_scales[0].bitcast(I32).rearrange("(q r) n -> r q n", r=4))
+        nc.scalar.dma_start(w_raw[:].bitcast(I32), w_words[0].bitcast(I32))
+        l1 = load_list(offs, "l1")
+        nc.scalar.dma_start(w0_raw[:].bitcast(I32), words8(w0_words))
+        l2 = load_list(offs2, "l2")
+        nc.scalar.dma_start(w_stage[:, :, 1, :], w0_scales[0].bitcast(I32).rearrange("(q r) n -> r q n", r=4))
+        xo_rows = xo_scales[0].bitcast(I32).rearrange("(h q r) n -> q r h n", h=2, q=2)
+        nc.sync.dma_start(xo_stage[64:68], xo_rows[0])
+        nc.scalar.dma_start(xt_win[:].bitcast(I32), words8(xt_words))
+        nc.sync.dma_start(xo_stage[96:100], xo_rows[1])
+        nc.scalar.dma_start(xo_win[:].bitcast(I32), xo_words[0].bitcast(I32))
+        for q in range(4):
+            nc.sync.dma_start(xt_plane[:].bitcast(I32)[q:P:32, :], lane_rows(xt_scales, q))
+        l3 = load_list(offs3, "l3")
+        l4 = load_list(offs4, "l4")
+        l5 = load_list(offs5, "l5")
+        l6 = load_list(offs6, "l6")
+        l7 = load_list(offs7, "l7")
+        boards = [tile([P, C], F32, "board%d" % t) for t in range(4)]
+        for t in range(4):
+            nc.vector.memset(boards[t][:], 0.0)
+
+        w_plane_words = w_plane[:].rearrange("p m n -> p (m n)").bitcast(I32)
+        for q in range(4):
+            nc.vector.tensor_copy(w_plane_words[32 * q : 32 * q + 4, :], w_stage[:, q, :, :].rearrange("p m n -> p (m n)"))
+        w_dealt = tile([P, 4, P], U16, "w_dealt")
+        w0_dealt = tile([P, 4, P], U32, "w0_dealt")
+        nc.scalar.copy(w_dealt[:], w_raw[:].rearrange("p (q t) -> p t q", t=4))
+        nc.scalar.copy(w0_dealt[:], w0_raw[:].rearrange("p (q t) -> p t q", t=4))
+        ws_dealt = tile([P, 2, 4, P], U8, "ws_dealt")
+        nc.vector.tensor_copy(ws_dealt[:], w_plane[:].rearrange("p m (q t) -> p m t q", t=4))
+        for h in range(2):
+            nc.vector.tensor_copy(xo_plane[:].bitcast(I32)[64 * h : 64 * h + 64, :], xo_stage[64:P, h, :])
+
+        sa_t = tile([P, 4], F32, "sa_t", "w_stage")
+        sb_t = tile([P, 4], F32, "sb_t", "w_raw")
+        nc.sync.dma_start(sa_t[:], sa.rearrange("(p t) o -> p (t o)", t=4))
+        nc.sync.dma_start(sb_t[:], sb.rearrange("(p t) o -> p (t o)", t=4))
+        vs_win = tile([P, S], U32, "vs_win", "w0_raw")
+        nc.sync.dma_start(vs_win[:].bitcast(I32), words8(vs_words))
+        vs_plane = tile([P, S], U8, "vs_plane", "w_plane")
+
+        a = [tile([P, J], F32, "a%d" % t) for t in range(4)]
+
+        def first_half(h):
+            cols = slice(h * H, (h + 1) * H)
+            lc = slice(h * H // 16, (h + 1) * H // 16)
+            xt_g = tile([P, H], U32, "xt_g")
+            xt_gs = tile([P, H], U8, "xt_gs")
+            xo_g = tile([P, H], U16, "xo_g")
+            xo_gs = tile([P, H], U8, "xo_gs")
+            nc.vector.tensor_copy(xt_g[:], xt_win[:].indirect(l1[:, lc]))
+            nc.vector.tensor_copy(xt_gs[:], xt_plane[:].indirect(l1[:, lc]))
+            nc.vector.tensor_copy(xo_gs[:], xo_plane[:].indirect(l2[:, lc]))
+            nc.vector.tensor_copy(xo_g[:], xo_win[:].indirect(l2[:, lc]))
+            for t in range(4):
+                acc = psum.tile([P, H], F32, name="acc%d" % (t + 4 * h * (t < 2)))
+                nc.tensor.matmul_mx(acc[:], lhsT=w_dealt[:, t, :].bitcast(E2M1), lhsT_scale=ws_dealt[:, 0, t, :],
+                                    rhs=xt_g[:].bitcast(E4M3), rhs_scale=xt_gs[:], start=True, stop=False)
+                nc.tensor.matmul_mx(acc[:], lhsT=w0_dealt[:, t, :].bitcast(E5M2), lhsT_scale=ws_dealt[:, 1, t, :],
+                                    rhs=xo_g[:].bitcast(E2M1), rhs_scale=xo_gs[:], start=False, stop=True)
+                if h == 0 and t == 0:
+                    nc.scalar.activation(a[t][:, cols], acc[:], COPY)
+                else:
+                    nc.vector.tensor_copy(a[t][:, cols], acc[:])
+
+        def place(t, h):
+            nc.scalar.activation(boards[t][:].indirect(l3[:, h * H // 16 : (h + 1) * H // 16]), a[t][:, h * H : (h + 1) * H], COPY)
+
+
+        def look(t):
+            x = tile([P, O], F32, "x%d" % t)
+            y = tile([P, O], F32, "y%d" % t)
+            nc.scalar.activation(x[:], boards[t][:].indirect(l4[:]), COPY, scale=sa_t[:, t : t + 1])
+            nc.scalar.activation(y[:], boards[t][:].indirect(l5[:]), COPY, scale=sb_t[:, t : t + 1])
+            nc.vector.tensor_tensor(diffs[t // 2][:, t % 2, :], x[:], y[:], ALU.subtract)
+            if t % 2 == 1:
+                pair = diffs[t // 2][:].rearrange("p t o -> p o t")
+                nc.vector.scalar_tensor_tensor(hid[:, :, t - 1 : t + 1], pair, -1.0, pair, ALU.mult, ALU.max)
+
+        first_half(0)
+        for t in range(4):
+            place(t, 0)
+        first_half(1)
+        nc.vector.memset(vs_plane[:].bitcast(I32), 0)
+        for q in range(4):
+            nc.sync.dma_start(vs_plane[:].bitcast(I32)[q:P:32, :], lane_rows(vs_scales, q))
+        pages = [tile([P, E], F32, "page%d" % u) for u in range(2)]
+        for u in range(2):
+            nc.gpsimd.memset(pages[u][:], 0.0)
+        vs_g = tile([P, N], U32, "vs_g")
+        vs_gs = tile([P, N], U8, "vs_gs")
+        nc.vector.tensor_copy(vs_g[:], vs_win[:].indirect(l6[:]))
+        nc.vector.tensor_copy(vs_gs[:], vs_plane[:].indirect(l6[:]))
+
+        hid = tile([P, O, 4], BF16, "hid", "w0_raw")
+        diffs = [tile([P, 2, O], F32, "diff0", "w_plane"), tile([P, 2, O], F32, "diff1")]
+        place(0, 1)
+        place(1, 1)
+        look(0)
+        place(2, 1)
+        look(1)
+        place(3, 1)
+        look(2)
+        look(3)
+
+        hid_q = tile([P, O], U32, "hid_q")
+        hid_s = tile([P, O], U8, "hid_s")
+        nc.vector.quantize_mx(hid_q[:].bitcast(E4M3), hid_s[:], hid[:].rearrange("p o t -> p (o t)"))
+        for u in range(2):
+            rows = slice(u * P, (u + 1) * P)
+            acc = psum.tile([P, O], F32, name="res%d" % u)
+            nc.tensor.matmul_mx(acc[:], lhsT=vs_g[:, rows].bitcast(E5M2), lhsT_scale=vs_gs[:, rows],
+                                rhs=hid_q[:].bitcast(E4M3), rhs_scale=hid_s[:], start=True, stop=True)
+            res = tile([P, O], F32, "res_sb%d" % u)
+            if u == 0:
+                nc.vector.tensor_copy(res[:], acc[:])
+                nc.vector.tensor_copy(pages[u][:].indirect(l7[:]), res[:])
+                nc.sync.dma_start(out[rows, :], pages[u][:])
+            else:
+                nc.scalar.copy(res[:], acc[:])
+                nc.scalar.activation(pages[u][:].indirect(l7[:]), res[:], COPY)
+                nc.scalar.dma_start(out[rows, :], pages[u][:])

@@ -64,11 +64,11 @@ def tile_list_ownboard_bank_store_scattered_kernel(
         nc.scalar.dma_start(w0_raw[:].bitcast(I32), words8(w0_words))
         l2 = load_list(offs2, "l2")
         nc.scalar.dma_start(w_stage[:, :, 1, :], w0_scales[0].bitcast(I32).rearrange("(q r) n -> r q n", r=4))
+        nc.sync.dma_start(xo_win[:].bitcast(I32), xo_words[0].bitcast(I32))
+        nc.scalar.dma_start(xt_win[:].bitcast(I32), words8(xt_words))
         xo_rows = xo_scales[0].bitcast(I32).rearrange("(h q r) n -> q r h n", h=2, q=2)
         nc.sync.dma_start(xo_stage[64:68], xo_rows[0])
-        nc.scalar.dma_start(xt_win[:].bitcast(I32), words8(xt_words))
         nc.sync.dma_start(xo_stage[96:100], xo_rows[1])
-        nc.scalar.dma_start(xo_win[:].bitcast(I32), xo_words[0].bitcast(I32))
         for q in range(4):
             nc.sync.dma_start(xt_plane[:].bitcast(I32)[q:P:32, :], lane_rows(xt_scales, q))
         l3 = load_list(offs3, "l3")
@@ -87,8 +87,14 @@ def tile_list_ownboard_bank_store_scattered_kernel(
         w0_dealt = tile([P, 4, P], U32, "w0_dealt")
         nc.scalar.copy(w_dealt[:], w_raw[:].rearrange("p (q t) -> p t q", t=4))
         nc.scalar.copy(w0_dealt[:], w0_raw[:].rearrange("p (q t) -> p t q", t=4))
-        ws_dealt = tile([P, 2, 4, P], U8, "ws_dealt")
-        nc.vector.tensor_copy(ws_dealt[:], w_plane[:].rearrange("p m (q t) -> p m t q", t=4))
+        ws_first = tile([P, 2, P], U8, "ws_first")
+        ws_rest = tile([P, 3, 2, P], U8, "ws_rest")
+        by_t = w_plane[:].rearrange("p m (q t) -> p t m q", t=4)
+        nc.vector.tensor_copy(ws_first[:], by_t[:, 0])
+
+        def w_scale(t, m):
+            return ws_first[:, m, :] if t == 0 else ws_rest[:, t - 1, m, :]
+
         for h in range(2):
             nc.vector.tensor_copy(xo_plane[:].bitcast(I32)[64 * h : 64 * h + 64, :], xo_stage[64:P, h, :])
 
@@ -109,16 +115,18 @@ def tile_list_ownboard_bank_store_scattered_kernel(
             xt_gs = tile([P, H], U8, "xt_gs")
             xo_g = tile([P, H], U16, "xo_g")
             xo_gs = tile([P, H], U8, "xo_gs")
-            nc.vector.tensor_copy(xt_g[:], xt_win[:].indirect(l1[:, lc]))
-            nc.vector.tensor_copy(xt_gs[:], xt_plane[:].indirect(l1[:, lc]))
-            nc.vector.tensor_copy(xo_gs[:], xo_plane[:].indirect(l2[:, lc]))
             nc.vector.tensor_copy(xo_g[:], xo_win[:].indirect(l2[:, lc]))
+            nc.vector.tensor_copy(xo_gs[:], xo_plane[:].indirect(l2[:, lc]))
+            nc.vector.tensor_copy(xt_gs[:], xt_plane[:].indirect(l1[:, lc]))
+            nc.vector.tensor_copy(xt_g[:], xt_win[:].indirect(l1[:, lc]))
+            if h == 0:
+                nc.vector.tensor_copy(ws_rest[:], by_t[:, 1:4])
             for t in range(4):
                 acc = psum.tile([P, H], F32, name="acc%d" % (t + 4 * h * (t < 2)))
-                nc.tensor.matmul_mx(acc[:], lhsT=w_dealt[:, t, :].bitcast(E2M1), lhsT_scale=ws_dealt[:, 0, t, :],
-                                    rhs=xt_g[:].bitcast(E4M3), rhs_scale=xt_gs[:], start=True, stop=False)
-                nc.tensor.matmul_mx(acc[:], lhsT=w0_dealt[:, t, :].bitcast(E5M2), lhsT_scale=ws_dealt[:, 1, t, :],
-                                    rhs=xo_g[:].bitcast(E2M1), rhs_scale=xo_gs[:], start=False, stop=True)
+                nc.tensor.matmul_mx(acc[:], lhsT=w0_dealt[:, t, :].bitcast(E5M2), lhsT_scale=w_scale(t, 1),
+                                    rhs=xo_g[:].bitcast(E2M1), rhs_scale=xo_gs[:], start=True, stop=False)
+                nc.tensor.matmul_mx(acc[:], lhsT=w_dealt[:, t, :].bitcast(E2M1), lhsT_scale=w_scale(t, 0),
+                                    rhs=xt_g[:].bitcast(E4M3), rhs_scale=xt_gs[:], start=False, stop=True)
                 if h == 0 and t == 0:
                     nc.scalar.activation(a[t][:, cols], acc[:], COPY)
                 else:
@@ -133,9 +141,9 @@ def tile_list_ownboard_bank_store_scattered_kernel(
             y = tile([P, O], F32, "y%d" % t)
             nc.scalar.activation(x[:], boards[t][:].indirect(l4[:]), COPY, scale=sa_t[:, t : t + 1])
             nc.scalar.activation(y[:], boards[t][:].indirect(l5[:]), COPY, scale=sb_t[:, t : t + 1])
-            nc.vector.tensor_tensor(diffs[t // 2][:, t % 2, :], x[:], y[:], ALU.subtract)
+            nc.vector.tensor_tensor(diffs[:, t, :], x[:], y[:], ALU.subtract)
             if t % 2 == 1:
-                pair = diffs[t // 2][:].rearrange("p t o -> p o t")
+                pair = diffs[:, t - 1 : t + 1, :].rearrange("p t o -> p o t")
                 nc.vector.scalar_tensor_tensor(hid[:, :, t - 1 : t + 1], pair, -1.0, pair, ALU.mult, ALU.max)
 
         first_half(0)
@@ -147,14 +155,14 @@ def tile_list_ownboard_bank_store_scattered_kernel(
             nc.sync.dma_start(vs_plane[:].bitcast(I32)[q:P:32, :], lane_rows(vs_scales, q))
         pages = [tile([P, E], F32, "page%d" % u) for u in range(2)]
         for u in range(2):
-            nc.gpsimd.memset(pages[u][:], 0.0)
+            nc.vector.memset(pages[u][:], 0.0)
         vs_g = tile([P, N], U32, "vs_g")
         vs_gs = tile([P, N], U8, "vs_gs")
         nc.vector.tensor_copy(vs_g[:], vs_win[:].indirect(l6[:]))
         nc.vector.tensor_copy(vs_gs[:], vs_plane[:].indirect(l6[:]))
 
-        hid = tile([P, O, 4], BF16, "hid", "w0_raw")
-        diffs = [tile([P, 2, O], F32, "diff0", "w_plane"), tile([P, 2, O], F32, "diff1")]
+        hid = tile([P, O, 4], BF16, "hid")
+        diffs = tile([P, 4, O], F32, "diffs", "w_plane")
         place(0, 1)
         place(1, 1)
         look(0)

@@ -60,12 +60,12 @@ def tile_list_ownboard_bank_store_scattered_kernel(
 
         nc.sync.dma_start(w_stage[:, :, 0, :], w_scales[0].bitcast(I32).rearrange("(q r) n -> r q n", r=4))
         nc.scalar.dma_start(w_raw[:].bitcast(I32), w_words[0].bitcast(I32))
-        l1 = load_list(offs, "l1")
+        nc.sync.dma_start(w_stage[:, :, 1, :], w0_scales[0].bitcast(I32).rearrange("(q r) n -> r q n", r=4))
         nc.scalar.dma_start(w0_raw[:].bitcast(I32), words8(w0_words))
+        l1 = load_list(offs, "l1")
         l2 = load_list(offs2, "l2")
-        nc.scalar.dma_start(w_stage[:, :, 1, :], w0_scales[0].bitcast(I32).rearrange("(q r) n -> r q n", r=4))
+        nc.sync.dma_start(xt_win[:].bitcast(I32), words8(xt_words))
         nc.sync.dma_start(xo_win[:].bitcast(I32), xo_words[0].bitcast(I32))
-        nc.scalar.dma_start(xt_win[:].bitcast(I32), words8(xt_words))
         xo_rows = xo_scales[0].bitcast(I32).rearrange("(h q r) n -> q r h n", h=2, q=2)
         nc.sync.dma_start(xo_stage[64:68], xo_rows[0])
         nc.sync.dma_start(xo_stage[96:100], xo_rows[1])
@@ -87,13 +87,12 @@ def tile_list_ownboard_bank_store_scattered_kernel(
         w0_dealt = tile([P, 4, P], U32, "w0_dealt")
         nc.scalar.copy(w_dealt[:], w_raw[:].rearrange("p (q t) -> p t q", t=4))
         nc.scalar.copy(w0_dealt[:], w0_raw[:].rearrange("p (q t) -> p t q", t=4))
-        ws_first = tile([P, 2, P], U8, "ws_first")
-        ws_rest = tile([P, 3, 2, P], U8, "ws_rest")
+        ws_dealt = tile([P, 4, 2, P], U8, "ws_dealt")
         by_t = w_plane[:].rearrange("p m (q t) -> p t m q", t=4)
-        nc.vector.tensor_copy(ws_first[:], by_t[:, 0])
+        nc.vector.tensor_copy(ws_dealt[:], by_t)
 
         def w_scale(t, m):
-            return ws_first[:, m, :] if t == 0 else ws_rest[:, t - 1, m, :]
+            return ws_dealt[:, t, m, :]
 
         for h in range(2):
             nc.vector.tensor_copy(xo_plane[:].bitcast(I32)[64 * h : 64 * h + 64, :], xo_stage[64:P, h, :])
@@ -104,7 +103,6 @@ def tile_list_ownboard_bank_store_scattered_kernel(
         nc.sync.dma_start(sb_t[:], sb.rearrange("(p t) o -> p (t o)", t=4))
         vs_win = tile([P, S], U32, "vs_win", "w0_raw")
         nc.sync.dma_start(vs_win[:].bitcast(I32), words8(vs_words))
-        vs_plane = tile([P, S], U8, "vs_plane", "w_plane")
 
         a = [tile([P, J], F32, "a%d" % t) for t in range(4)]
 
@@ -115,18 +113,16 @@ def tile_list_ownboard_bank_store_scattered_kernel(
             xt_gs = tile([P, H], U8, "xt_gs")
             xo_g = tile([P, H], U16, "xo_g")
             xo_gs = tile([P, H], U8, "xo_gs")
+            nc.vector.tensor_copy(xt_g[:], xt_win[:].indirect(l1[:, lc]))
             nc.vector.tensor_copy(xo_g[:], xo_win[:].indirect(l2[:, lc]))
             nc.vector.tensor_copy(xo_gs[:], xo_plane[:].indirect(l2[:, lc]))
             nc.vector.tensor_copy(xt_gs[:], xt_plane[:].indirect(l1[:, lc]))
-            nc.vector.tensor_copy(xt_g[:], xt_win[:].indirect(l1[:, lc]))
-            if h == 0:
-                nc.vector.tensor_copy(ws_rest[:], by_t[:, 1:4])
             for t in range(4):
                 acc = psum.tile([P, H], F32, name="acc%d" % (t + 4 * h * (t < 2)))
-                nc.tensor.matmul_mx(acc[:], lhsT=w0_dealt[:, t, :].bitcast(E5M2), lhsT_scale=w_scale(t, 1),
-                                    rhs=xo_g[:].bitcast(E2M1), rhs_scale=xo_gs[:], start=True, stop=False)
                 nc.tensor.matmul_mx(acc[:], lhsT=w_dealt[:, t, :].bitcast(E2M1), lhsT_scale=w_scale(t, 0),
-                                    rhs=xt_g[:].bitcast(E4M3), rhs_scale=xt_gs[:], start=False, stop=True)
+                                    rhs=xt_g[:].bitcast(E4M3), rhs_scale=xt_gs[:], start=True, stop=False)
+                nc.tensor.matmul_mx(acc[:], lhsT=w0_dealt[:, t, :].bitcast(E5M2), lhsT_scale=w_scale(t, 1),
+                                    rhs=xo_g[:].bitcast(E2M1), rhs_scale=xo_gs[:], start=False, stop=True)
                 if h == 0 and t == 0:
                     nc.scalar.activation(a[t][:, cols], acc[:], COPY)
                 else:
@@ -150,19 +146,20 @@ def tile_list_ownboard_bank_store_scattered_kernel(
         for t in range(4):
             place(t, 0)
         first_half(1)
+        vs_plane = tile([P, S], U8, "vs_plane", "xt_plane")
         nc.vector.memset(vs_plane[:].bitcast(I32), 0)
         for q in range(4):
             nc.sync.dma_start(vs_plane[:].bitcast(I32)[q:P:32, :], lane_rows(vs_scales, q))
         pages = [tile([P, E], F32, "page%d" % u) for u in range(2)]
         for u in range(2):
             nc.vector.memset(pages[u][:], 0.0)
-        vs_g = tile([P, N], U32, "vs_g")
-        vs_gs = tile([P, N], U8, "vs_gs")
+        vs_g = tile([P, N], U32, "vs_g", "xt_g")
+        vs_gs = tile([P, N], U8, "vs_gs", "xt_gs")
         nc.vector.tensor_copy(vs_g[:], vs_win[:].indirect(l6[:]))
         nc.vector.tensor_copy(vs_gs[:], vs_plane[:].indirect(l6[:]))
 
         hid = tile([P, O, 4], BF16, "hid")
-        diffs = tile([P, 4, O], F32, "diffs", "w_plane")
+        diffs = tile([P, 4, O], F32, "diffs", "xt_plane")
         place(0, 1)
         place(1, 1)
         look(0)

from contextlib import ExitStack

import concourse.mybir as mybir

F32 = mybir.dt.float32
BF16 = mybir.dt.bfloat16
I32 = mybir.dt.int32
U32 = mybir.dt.uint32
U16 = mybir.dt.uint16
U8 = mybir.dt.uint8
E4M3 = mybir.dt.float8_e4m3fn_x4
E5M2 = mybir.dt.float8_e5m2_x4
E2M1 = mybir.dt.float4_e2m1fn_x4
COPY = mybir.ActivationFunctionType.Copy
ALU = mybir.AluOpType

P = 128
K, T, J, R, F, Z, C, O, N, S, E = 512, 1024, 256, 512, 512, 1024, 512, 128, 256, 1024, 1024
FLOPS = 2 * K * R * J + 2 * F * R * J + 2 * R * N * O
H = J // 2


def tile_list_ownboard_bank_store_scattered_kernel(
    tc, xt_words, xt_scales, xo_words, xo_scales, w_words, w_scales, w0_words, w0_scales,
    sa, sb, vs_words, vs_scales, offs, offs2, offs3, offs4, offs5, offs6, offs7, out
):
    nc = tc.nc
    with ExitStack() as ctx:
        lists = ctx.enter_context(tc.tile_pool(name="lists", bufs=1))
        sb_pool = ctx.enter_context(tc.tile_pool(name="sbuf", bufs=1))
        psum = ctx.enter_context(tc.psum_pool(name="psum", bufs=1))

        def tile(shape, dtype, name, tag=None):
            return sb_pool.tile(shape, dtype, name=name, tag=tag or name, align_bytes=64)

        def load_list(src, name):
            t = lists.tile(list(src.shape), U16, name=name)
            nc.sync.dma_start(t[:], src)
            return t

        def words8(src):
            return src[0].rearrange("p n b -> p (n b)").bitcast(I32)

        def lane_rows(src, r):
            return src[0].bitcast(I32)[r:16:4, :]

        xo_stage = tile([P, 2, Z // 4], I32, "xo_stage")
        xt_plane = tile([P, T], U8, "xt_plane")
        xo_plane = tile([P, Z], U8, "xo_plane")
        w_plane = tile([P, 2, R], U8, "w_plane")
        nc.vector.memset(xo_stage[64:P], 0)
        nc.vector.memset(xt_plane[:].bitcast(I32), 0)
        nc.vector.memset(w_plane[:].bitcast(I32), 0)

        w_raw = tile([P, R], U16, "w_raw")
        w0_raw = tile([P, R], U32, "w0_raw")
        xt_win = tile([P, T], U32, "xt_win", "page0")
        xo_win = tile([P, Z], U16, "xo_win", "page1")
        w_stage = tile([4, 4, 2, R // 4], I32, "w_stage")

        nc.sync.dma_start(w_stage[:, :, 0, :], w_scales[0].bitcast(I32).rearrange("(q r) n -> r q n", r=4))
        nc.scalar.dma_start(w_raw[:].bitcast(I32), w_words[0].bitcast(I32))
        nc.sync.dma_start(w_stage[:, :, 1, :], w0_scales[0].bitcast(I32).rearrange("(q r) n -> r q n", r=4))
        nc.scalar.dma_start(w0_raw[:].bitcast(I32), words8(w0_words))
        l1 = load_list(offs, "l1")
        l2 = load_list(offs2, "l2")
        nc.sync.dma_start(xt_win[:].bitcast(I32), words8(xt_words))
        nc.sync.dma_start(xo_win[:].bitcast(I32), xo_words[0].bitcast(I32))
        xo_rows = xo_scales[0].bitcast(I32).rearrange("(h q r) n -> q r h n", h=2, q=2)
        nc.sync.dma_start(xo_stage[64:68], xo_rows[0])
        nc.sync.dma_start(xo_stage[96:100], xo_rows[1])
        for q in range(4):
            nc.sync.dma_start(xt_plane[:].bitcast(I32)[q:P:32, :], lane_rows(xt_scales, q))
        l3 = load_list(offs3, "l3")
        l4 = load_list(offs4, "l4")
        l5 = load_list(offs5, "l5")
        l6 = load_list(offs6, "l6")
        l7 = load_list(offs7, "l7")
        boards = [tile([P, C], F32, "board%d" % t) for t in range(4)]
        for t in range(4):
            nc.vector.memset(boards[t][:], 0.0)

        w_plane_words = w_plane[:].rearrange("p m n -> p (m n)").bitcast(I32)
        for q in range(4):
            nc.vector.tensor_copy(w_plane_words[32 * q : 32 * q + 4, :], w_stage[:, q, :, :].rearrange("p m n -> p (m n)"))
        w_dealt = tile([P, 4, P], U16, "w_dealt")
        w0_dealt = tile([P, 4, P], U32, "w0_dealt")
        nc.scalar.copy(w_dealt[:], w_raw[:].rearrange("p (q t) -> p t q", t=4))
        nc.scalar.copy(w0_dealt[:], w0_raw[:].rearrange("p (q t) -> p t q", t=4))
        ws_dealt = tile([P, 4, 2, P], U8, "ws_dealt")
        by_t = w_plane[:].rearrange("p m (q t) -> p t m q", t=4)
        nc.vector.tensor_copy(ws_dealt[:], by_t)

        def w_scale(t, m):
            return ws_dealt[:, t, m, :]

        for h in range(2):
            nc.vector.tensor_copy(xo_plane[:].bitcast(I32)[64 * h : 64 * h + 64, :], xo_stage[64:P, h, :])

        sa_t = tile([P, 4], F32, "sa_t", "w_stage")
        sb_t = tile([P, 4], F32, "sb_t", "w_raw")
        nc.sync.dma_start(sa_t[:], sa.rearrange("(p t) o -> p (t o)", t=4))
        nc.sync.dma_start(sb_t[:], sb.rearrange("(p t) o -> p (t o)", t=4))
        vs_win = tile([P, S], U32, "vs_win", "w0_raw")
        nc.sync.dma_start(vs_win[:].bitcast(I32), words8(vs_words))

        a = [tile([P, J], F32, "a%d" % t) for t in range(4)]

        def first_half(h):
            cols = slice(h * H, (h + 1) * H)
            lc = slice(h * H // 16, (h + 1) * H // 16)
            xt_g = tile([P, H], U32, "xt_g")
            xt_gs = tile([P, H], U8, "xt_gs")
            xo_g = tile([P, H], U16, "xo_g")
            xo_gs = tile([P, H], U8, "xo_gs")
            nc.vector.tensor_copy(xt_g[:], xt_win[:].indirect(l1[:, lc]))
            nc.vector.tensor_copy(xo_g[:], xo_win[:].indirect(l2[:, lc]))
            nc.vector.tensor_copy(xo_gs[:], xo_plane[:].indirect(l2[:, lc]))
            nc.vector.tensor_copy(xt_gs[:], xt_plane[:].indirect(l1[:, lc]))
            for t in range(4):
                acc = psum.tile([P, H], F32, name="acc%d" % (t + 4 * h * (t < 2)))
                nc.tensor.matmul_mx(acc[:], lhsT=w_dealt[:, t, :].bitcast(E2M1), lhsT_scale=w_scale(t, 0),
                                    rhs=xt_g[:].bitcast(E4M3), rhs_scale=xt_gs[:], start=True, stop=False)
                nc.tensor.matmul_mx(acc[:], lhsT=w0_dealt[:, t, :].bitcast(E5M2), lhsT_scale=w_scale(t, 1),
                                    rhs=xo_g[:].bitcast(E2M1), rhs_scale=xo_gs[:], start=False, stop=True)
                if h == 0 and t == 0:
                    nc.scalar.activation(a[t][:, cols], acc[:], COPY)
                else:
                    nc.vector.tensor_copy(a[t][:, cols], acc[:])

        def place(t, h):
            nc.scalar.activation(boards[t][:].indirect(l3[:, h * H // 16 : (h + 1) * H // 16]), a[t][:, h * H : (h + 1) * H], COPY)


        def look(t):
            x = tile([P, O], F32, "x%d" % t)
            y = tile([P, O], F32, "y%d" % t)
            nc.scalar.activation(x[:], boards[t][:].indirect(l4[:]), COPY, scale=sa_t[:, t : t + 1])
            nc.scalar.activation(y[:], boards[t][:].indirect(l5[:]), COPY, scale=sb_t[:, t : t + 1])
            nc.vector.tensor_tensor(diffs[:, t, :], x[:], y[:], ALU.subtract)
            if t % 2 == 1:
                pair = diffs[:, t - 1 : t + 1, :].rearrange("p t o -> p o t")
                nc.vector.scalar_tensor_tensor(hid[:, :, t - 1 : t + 1], pair, -1.0, pair, ALU.mult, ALU.max)

        first_half(0)
        for t in range(4):
            place(t, 0)
        first_half(1)
        vs_plane = tile([P, S], U8, "vs_plane", "xt_plane")
        nc.vector.memset(vs_plane[:].bitcast(I32), 0)
        for q in range(4):
            nc.sync.dma_start(vs_plane[:].bitcast(I32)[q:P:32, :], lane_rows(vs_scales, q))
        pages = [tile([P, E], F32, "page%d" % u) for u in range(2)]
        for u in range(2):
            nc.vector.memset(pages[u][:], 0.0)
        vs_g = tile([P, N], U32, "vs_g", "xt_g")
        vs_gs = tile([P, N], U8, "vs_gs", "xt_gs")
        nc.vector.tensor_copy(vs_g[:], vs_win[:].indirect(l6[:]))
        nc.vector.tensor_copy(vs_gs[:], vs_plane[:].indirect(l6[:]))

        hid = tile([P, O, 4], BF16, "hid")
        diffs = tile([P, 4, O], F32, "diffs", "xt_plane")
        place(0, 1)
        place(1, 1)
        look(0)
        place(2, 1)
        look(1)
        place(3, 1)
        look(2)
        look(3)

        hid_q = tile([P, O], U32, "hid_q")
        hid_s = tile([P, O], U8, "hid_s")
        nc.vector.quantize_mx(hid_q[:].bitcast(E4M3), hid_s[:], hid[:].rearrange("p o t -> p (o t)"))
        for u in range(2):
            rows = slice(u * P, (u + 1) * P)
            acc = psum.tile([P, O], F32, name="res%d" % u)
            nc.tensor.matmul_mx(acc[:], lhsT=vs_g[:, rows].bitcast(E5M2), lhsT_scale=vs_gs[:, rows],
                                rhs=hid_q[:].bitcast(E4M3), rhs_scale=hid_s[:], start=True, stop=True)
            res = tile([P, O], F32, "res_sb%d" % u)
            if u == 0:
                nc.vector.tensor_copy(res[:], acc[:])
                nc.vector.tensor_copy(pages[u][:].indirect(l7[:]), res[:])
                nc.sync.dma_start(out[rows, :], pages[u][:])
            else:
                nc.scalar.copy(res[:], acc[:])
                nc.scalar.activation(pages[u][:].indirect(l7[:]), res[:], COPY)
                nc.scalar.dma_start(out[rows, :], pages[u][:])
